import numpy as np, ml_dtypes
CORES = [9,25,41,57]
N = 4
import mx_ref
BF = ml_dtypes.bfloat16
def cols(t, e):
    v = np.concatenate([t.reshape(128, -1, 4), np.zeros((128, 1, 4), BF)], axis=1)
    return np.ascontiguousarray(v[:, e]).reshape(128, -1)
def cut(t, i, w=512):
    return t[:, w * i:w * i + w]
def f(rng, *shape):
    return mx_ref.flush((rng.standard_normal(shape, dtype=np.float32) * np.exp2(rng.integers(-2, 3, shape[:-1] + (1,)))).astype(BF))
def wide(rng, *shape, cols=0):
    v = rng.standard_normal(shape, dtype=np.float32) * np.exp2(rng.integers(-12, 13, shape)).astype(np.float32)
    if cols: v *= np.repeat(np.exp2(rng.integers(-cols, cols + 1, shape[:-2] + (1, shape[-1] // 4))) * (rng.random(shape[:-2] + (1, shape[-1] // 4)) > 0.0625), 4, axis=-1).astype(np.float32)
    return mx_ref.flush(v.astype(BF))
P, K, R, O = 512, 32, 4, 2
def bf(v):
    return mx_ref.flush(np.asarray(v, np.float32).astype(BF))
def same(v):
    t = np.zeros((128, 512), BF)
    t[:, :4] = v
    return np.stack([t] * N)
def setup_inputs(rng):
    return {"x": f(rng, N, 128, 4 * P), "u": same(f(rng, 128, 4)), "w": f(rng, N, 128, 512 * O)}
def setup_inputs_ties(rng):
    d = setup_inputs(rng)
    T = (P - K - 1) // 3
    H = T // 2
    shared = f(rng, 128, 4 * H)
    x = []
    for r in range(N):
        pool = np.concatenate([shared, f(rng, 128, 4 * (T + 1 - H))], axis=1)
        e = np.concatenate([np.repeat(np.arange(T), 3), np.full(P - 3 * T, T)])
        x.append(cols(pool, rng.permutation(e)))
    d["x"] = np.stack(x)
    d["u"] = bf(d["u"].astype(np.float32) * np.float32(256))
    return d
def setup_inputs_like(rng):
    d = setup_inputs(rng)
    at = rng.permutation(8)
    size = np.zeros(8)
    size[at] = np.exp2(-3.0 - np.arange(8) // 2)
    d["u"] = same(bf((1 + 0.25 * rng.random((128, 4))) * np.repeat(size, 16)[:, None]))
    side = rng.permutation(N) % 2
    x = []
    for r in range(N):
        c = rng.permutation(np.arange(P) % 8)
        h = np.where(c % 2 == side[r], 1.0, 0.75)
        on = np.repeat(np.arange(8)[:, None] == at[c][None, :], 16, axis=0) * h[None, :]
        x.append(bf((on[:, :, None] * (1 + 0.25 * rng.random((128, P, 4))) + 2.0 ** -8 * rng.standard_normal((128, P, 4))).reshape(128, 4 * P)))
    d["x"] = np.stack(x)
    return d
def setup_inputs_late(rng):
    d = setup_inputs(rng)
    half = (np.arange(128) < 64) ^ bool(rng.integers(0, 2))
    d["u"] = same(bf(2.0 ** 28 * (R - 1.5) * (1 + 0.25 * rng.random((128, 4))) * half[:, None]))
    x = []
    for r in range(N):
        late = rng.permutation(P) < rng.integers(2 * K, P // 2 + 1)
        v = np.where(half, 2.0 ** 22, 2.0 ** 26)[:, None] * np.where(late, -1.0, 1.0)[None, :]
        x.append(bf((v[:, :, None] * (1 + 0.25 * rng.random((128, P, 4)))).reshape(128, 4 * P)))
    d["x"] = np.stack(x)
    return d
def setup_inputs_low(rng):
    d = setup_inputs(rng)
    size = np.full((N, P), 2.0 ** 29)
    for r in range(N):
        e = 32 * int(rng.integers(0, P // 32)) + rng.permutation(32)[:K]
        size[r, e] = 2.0 ** 28
        size[r, e[:int(rng.integers(2, K // 2 + 1))]] = 0
    d["x"] = bf(np.repeat(size, 4, axis=1)[:, None, :] * (1.5 + 0.45 * rng.random((N, 128, 4 * P))))
    d["u"] = same(bf(-2.0 ** 29 * (1.5 + 0.45 * rng.random((128, 4)))))
    return d
def setup_inputs_spread(rng):
    d = setup_inputs(rng)
    d["x"] = wide(rng, N, 128, 4 * P, cols=6)
    d["u"] = same(bf(wide(rng, 128, 4).astype(np.float32) * np.float32(256)))
    return d
def check_inputs(d):
    b = []
    for k in ("x", "u", "w"):
        v = np.abs(d[k].astype(np.float32))
        if not (np.isfinite(v).all() and ((v == 0) | (v >= 2.0 ** -30) & (v <= 2.0 ** 30)).all()): b.append("a value of " + k)
    v = d["u"].astype(np.float32)
    if (v[:, :, 4:] != 0).any(): b.append("u has numbers behind its first column")
    if (v != v[:1]).any(): b.append("u isn't the same on all ranks")
    return b
def reference(x, u, w):
    X = [mx_ref.quantize(np.ascontiguousarray(x[r])) for r in range(N)]
    s = [mx_ref.matmul(mx_ref.quantize(np.ascontiguousarray(u[r])), X[r])[0] + np.float32(0.0) for r in range(N)]
    free = np.ones((N, P), bool)
    ch, se, y = np.zeros((N, R, K), np.float32), np.zeros((N, 1, P), np.float32), np.zeros((N, 128, O * R * 128), np.float32)
    M = []
    for b in range(R):
        best = []
        for r in range(N):
            e = np.argsort(np.where(free[r], -s[r], np.float32(np.inf)), kind="stable")[:K]
            free[r, e] = False
            ch[r, b] = e
            best.append(cols(x[r], e))
        M.append(mx_ref.quantize(np.ascontiguousarray(np.concatenate(best, axis=1))))
        if b < R - 1:
            for r in range(N):
                m = mx_ref.matmul(M[b], X[r]).max(axis=0) + np.float32(0.0)
                s[r] = s[r] - np.float32(0.25) * m
    for r in range(N):
        se[r, 0] = s[r]
        for o in range(O):
            q = mx_ref.quantize(np.ascontiguousarray(cut(w[r], o)))
            for b in range(R):
                i = (o * R + b) * 128
                y[r, :, i:i + 128] = mx_ref.matmul(q, M[b])
    return {"ch": ch, "se": se, "y": y}

@@ -1,0 +1,329 @@
+from concourse.bass import DstId, RemoteDMATransfer
+from concourse.mybir import dt, AluOpType, AxisListType, ActivationFunctionType
+
+OP = AluOpType
+P, K, R, O, N = 512, 32, 4, 2, 4
+CW = 640
+LW = 258
+KAPPA = 2.0 ** -24 * (1.0 + 2.0 ** -10)
+TINY = 2.0 ** -124
+BIG = 9e29
+GONE = -1e29
+
+X4 = "float8_e4m3fn_x4"
+SCRATCH = {
+    "uc": ("sbuf", [128, 4], "bfloat16"),
+    "ones": ("sbuf", [128, 128], "bfloat16"),
+    "ut": ("sbuf", [128, 512], "bfloat16"),
+    "uq": ("sbuf", [128, 128], X4),
+    "us": ("sbuf", [128, 128], "uint8"),
+    "xr": ("sbuf", [128, 4 * P], "bfloat16"),
+    "xp": ("sbuf", [128, 4 * P], "bfloat16"),
+    "xq": ("sbuf", [128, P], X4),
+    "xs": ("sbuf", [128, P], "uint8"),
+    "pq": ("sbuf", [128, P], X4),
+    "ps": ("sbuf", [128, P], "uint8"),
+    "wr": ("sbuf", [128, 512 * O], "bfloat16"),
+    "wq": ("sbuf", [128, 128 * O], X4),
+    "ws": ("sbuf", [128, 128 * O], "uint8"),
+    "mq": ("sbuf", [128, 128 * R], X4),
+    "ms": ("sbuf", [128, 128 * R], "uint8"),
+    "onef": ("sbuf", [128, 4], "float32"),
+    "big": ("sbuf", [128, 128], "float32"),
+    "mask": ("sbuf", [128, 128], "float32"),
+    "mg": ("sbuf", [128, 4], "float32"),
+    "quart": ("sbuf", [128, 32], "float32"),
+    "i16": ("sbuf", [128, 128], "bfloat16"),
+    "w16": ("sbuf", [128, 8], "int32"),
+    "wand": ("sbuf", [128, 8], "int32"),
+    "nl": ("sbuf", [128, 8], "bfloat16"),
+    "nh": ("sbuf", [128, 8], "bfloat16"),
+    "bc": ("sbuf", [128, 128 * R], "float32"),
+    "srt": ("sbuf", [128, 128 * R], "float32"),
+    "srh": ("sbuf", [128, 128 * R], "float32"),
+    "row": ("sbuf", [128, P * R], "float32"),
+    "dd": ("sbuf", [128, 4 * R], "float32"),
+    "thr": ("sbuf", [128, 16 * R], "float32"),
+    "cmp": ("sbuf", [128, CW * 4 * R], "bfloat16"),
+    "sc1": ("sbuf", [128, 256 * 4 * R], "bfloat16"),
+    "sc2": ("sbuf", [128, 64 * 4 * R], "bfloat16"),
+    "fl": ("sbuf", [128, 16 * R], "bfloat16"),
+    "ab": ("sbuf", [128, 4 * LW * R], "bfloat16"),
+    "abq": ("sbuf", [128, LW * R], X4),
+    "abs": ("sbuf", [128, LW * R], "uint8"),
+    "off": ("sbuf", [128, 2 * R], "uint16"),
+    "lst": ("sbuf", [128, 2 * R], "float32"),
+    "pen": ("sbuf", [128, 4 * R], "float32"),
+    "srp": ("sbuf", [128, 4 * R], "float32"),
+    "mx": ("sbuf", [128, 4 * R], "float32"),
+    "mq4": ("sbuf", [128, 4 * R], "float32"),
+    "st": ("sbuf", [128, 4 * R], "float32"),
+    "ysb": ("sbuf", [128, O * P], "float32"),
+    "psc": ("psum", [128, 2048], "float32"),
+    "psr": ("psum", [128, 1024], "float32"),
+    "psy": ("psum", [128, 1024], "float32"),
+}
+SEMAPHORES = ["sv", "ss", "sp", "sg", "du", "dx0", "dx1", "dx2", "dx3", "dw", "dout",
+              "arr0", "arr1", "arr2", "arr3", "loc"]
+
+
+def rank_program(g, core, T, topo):
+    rank = T.rank_of(core)
+    if rank is None:
+        return
+    AF = ActivationFunctionType
+    queue = {"V": g.vector, "S": g.scalar, "P": g.tensor, "G": g, "Y": g.sync}
+    own = {"V": "sv", "S": "ss", "P": "sp", "G": "sg"}
+    count, seen = {}, {}
+
+    def need(e, deps):
+        for s, v in deps:
+            if seen.get((e, s), 0) < v:
+                queue[e].wait_ge(T.sem[s], v)
+                seen[(e, s)] = v
+
+    def done(e, ins):
+        s = own[e]
+        count[s] = count.get(s, 0) + 1
+        ins.then_inc(T.sem[s], 1)
+        return (s, count[s])
+
+    def dma(e, out, in_, sem, deps=()):
+        need(e, deps)
+        count[sem] = count.get(sem, 0) + 16
+        queue[e].dma_start(out, in_).then_inc(T.sem[sem], 16)
+        return (sem, count[sem])
+
+    def ts(deps, out, in0, s1, s2, op0, op1=None):
+        need("V", deps)
+        if op1 is None:
+            return done("V", g.vector.tensor_scalar(out, in0, s1, s2, op0))
+        return done("V", g.vector.tensor_scalar(out, in0, s1, s2, op0, op1))
+
+    def tt(deps, out, in0, in1, op):
+        need("V", deps)
+        return done("V", g.vector.tensor_tensor(out, in0, in1, op))
+
+    def cp(deps, out, in_):
+        need("V", deps)
+        return done("V", g.vector.tensor_copy(out, in_))
+
+    def act(deps, out, in_, func, **kw):
+        need("S", deps)
+        return done("S", g.scalar.activation(out, in_, func, **kw))
+
+    def gneed(deps):
+        need("G", list(deps) + ([("sg", count["sg"])] if "sg" in count else []))
+
+    def fill(ap, v):
+        return done("V", g.vector.memset(ap, v))
+
+    def quant(deps, q, s, a, n, src, sa):
+        need("V", deps)
+        return done("V", g.vector.quantize_mx(q[:, a:a + n], s[:, a:a + n], src[:, sa:sa + 4 * n]))
+
+    def mm(deps, out, l, lq, ls, r, rq, rs, n, start=True, stop=True):
+        need("P", deps)
+        return done("P", g.tensor.matmul_mx(out, lq[:, l:l + 128], ls[:, l:l + 128],
+                                            rq[:, r:r + n], rs[:, r:r + n], start, stop))
+
+    du = dma("Y", T.uc[:], T.u[:, 0:4], "du")
+    dx = [None] * 4
+    for a in range(4):
+        dx[a] = dma("SYSY"[a], T.xr[:, 512 * a:512 * a + 512], T.x[:, 512 * a:512 * a + 512], "dx%d" % a)
+    dw = dma("Y", T.wr[:], T.w[:], "dw")
+
+    t_ones = fill(T.ones[:], 1.0)
+    t_onef = fill(T.onef[:], 1.0)
+    t_big = fill(T.big[:], BIG)
+    t_quart = fill(T.quart[:], -0.25)
+    for a in range(4):
+        gneed([])
+        t_w16 = done("G", g.iota(T.w16[32 * a:32 * a + 32, :], [[0, 2], [32, 4]], 128 * a + 16, 1))
+    gneed([t_onef])
+    t_mg = done("G", g.affine_select(T.mg[:], T.onef[:], [[32, 4]], OP.is_gt, 0.0, 0, -1))
+    for a in range(4):
+        gneed([t_big])
+        v = slice(32 * a, 32 * a + 32)
+        t_mask = done("G", g.affine_select(T.mask[v, :], T.big[v, :], [[0, 4], [1, 32]], OP.is_ge, -BIG, 0, -1))
+    gneed([])
+    t_i16 = done("G", g.iota(T.i16[:], [[0, 8], [1, 16]], 0, 0, allow_small_or_imprecise_dtypes=True))
+    for b in range(R):
+        t_ab0 = fill(T.ab[:, 4 * LW * b + 528:4 * LW * b + 4 * LW], 0.0)
+    t_wand = ts([t_w16], T.wand[:], T.w16[:], 31, None, OP.bitwise_and)
+    t_nl = ts([t_wand], T.nl[:], T.wand[:], 16, None, OP.subtract)
+    t_nh = tt([t_wand, t_w16], T.nh[:], T.w16[:], T.wand[:], OP.subtract)
+
+    for t in range(4):
+        t_ut = ts([du, t_ones], T.ut[:, t:512:4], T.ones[:], T.uc[:, t:t + 1], None, OP.mult)
+    t_uq = quant([t_ut], T.uq, T.us, 0, 128, T.ut, 0)
+
+    t_xq, t_cv, t_cs, t_row = [None] * 4, None, None, [None] * 2
+    for a in range(4):
+        for c in range(4):
+            out = T.xp[:, 512 * c + 128 * a:512 * c + 128 * a + 128]
+            in_ = T.xr[:, 512 * a + 128 * c:512 * a + 128 * c + 128]
+            if c < 2:
+                t_cv = cp([dx[a]], out, in_)
+            else:
+                t_cs = act([dx[a]], out, in_, AF.Copy)
+        t_xq[a] = quant([dx[a]], T.xq, T.xs, 128 * a, 128, T.xr, 512 * a)
+        if a % 2:
+            h = a // 2
+            t_row[h] = mm([t_xq[a], t_uq], T.psr[:, 512 * h:512 * h + 256], 0, T.uq, T.us, 256 * h, T.xq, T.xs, 256)
+    t_pq, t_col = [None] * 4, [None] * 4
+    for c in range(4):
+        t_pq[c] = quant([t_cv if c < 2 else t_cs], T.pq, T.ps, 128 * c, 128, T.xp, 512 * c)
+        t_col[c] = mm([t_pq[c], t_uq], T.psc[:, 512 * c:512 * c + 128], 128 * c, T.pq, T.ps, 0, T.uq, T.us, 128)
+    for c in range(4):
+        t_bc = cp([t_col[c]], T.bc[:, 32 * c:32 * c + 32], T.psc[:, 512 * c:512 * c + 32])
+    free_c = [t_bc] * 4
+
+    dests = [c for c in T.cores if c != core]
+    mask = topo.mask(core, dests[0])
+    ids = []
+    for c in dests:
+        mask &= topo.mask(core, c)
+        rid, pid, _ = topo.addr(c)
+        ids.append(DstId(rid=rid, pnc=pid))
+    engs = bin(mask).count("1")
+
+    def send(view, b):
+        g.remote_dma_fused([RemoteDMATransfer(dst_ids=ids, dma_engine_mask=mask, remote_sem=T.sem["arr%d" % b],
+                                              srcs=[view], dsts=[view] * len(ids))], local_sem=T.sem.loc)
+
+    t_wq = t_st = t_m = t_srp = None
+    free_y = [None] * O
+    outs = []
+    for b in range(R):
+        B = 128 * b
+        need("V", [t_bc])
+        t_srt = done("V", g.vector.transpose(T.srt[:, B:B + 128], T.bc[:, B:B + 128]))
+        t_d = act([t_bc], T.dd[:, 4 * b:4 * b + 4], T.bc[:, B:B + 128:32], AF.Abs, bias=TINY, scale=KAPPA)
+        t_pb = [None] * 4
+        if b:
+            for a in range(4):
+                gneed([t_srt])
+                t_pb[a] = done("G", g.partition_broadcast(T.row[:, P * b + 128 * a:P * b + 128 * a + 128],
+                                                          T.srt[32 * a:32 * a + 1, B:B + 128], 128))
+        sc = [T.bc[:, B + 32 * c:B + 32 * c + 1] for c in range(4)]
+        at = [CW * (4 * b + c) for c in range(4)]
+        t_srh = tt([t_srt, t_mask], T.srh[:, B:B + 128], T.srt[:, B:B + 128], T.mask[:], OP.min)
+        for c in range(3):
+            ts([], T.cmp[:, at[c] + 32:at[c] + 128 - 32 * c], T.srt[:, B + 32 * c + 32:B + 128], sc[c], -1.0,
+               OP.is_equal, OP.mult)
+        for c in range(4):
+            ts([t_srh], T.cmp[:, at[c]:at[c] + 32], T.srh[:, B + 32 * c:B + 32 * c + 32], sc[c], -1.0,
+               OP.is_equal, OP.mult)
+        for c in range(4):
+            t_thr = ts([t_d, t_mg], T.thr[:, 16 * b + 4 * c:16 * b + 4 * c + 4], T.mg[:], T.dd[:, 4 * b + c:4 * b + c + 1],
+                       sc[c], OP.mult, OP.add)
+
+        def compare(a, c):
+            if b:
+                row, dep = T.row[:, P * b + 128 * a:P * b + 128 * a + 128], t_pb[a]
+            else:
+                row, dep = T.psr[:, 512 * (a // 2) + 128 * (a % 2):512 * (a // 2) + 128 * (a % 2) + 128], t_row[a // 2]
+            o = at[c] + 128 - 32 * c + 128 * a
+            i = 16 * b + 4 * c + a
+            return ts([t_thr, dep], T.cmp[:, o:o + 128], row, T.thr[:, i:i + 1], None, OP.is_ge)
+
+        for a in range(3):
+            for c in range(4):
+                t_c = compare(a, c)
+        t_s1 = [None] * 4
+        need("V", [t_c])
+        for c in range(4):
+            n = 256 - 16 * c
+            o1 = 256 * (4 * b + c)
+            t_s1[c] = done("V", g.vector.tensor_tensor_scan(T.sc1[:, o1:o1 + n], T.cmp[:, at[c]:at[c] + n],
+                                                            T.cmp[:, at[c] + n:at[c] + 2 * n], 0.0, OP.add, OP.add))
+        t_c3 = [compare(3, c) for c in range(4)]
+        for c in range(4):
+            n = 256 - 16 * c
+            o1 = 256 * (4 * b + c) + n - 1
+            o2 = 64 * (4 * b + c)
+            need("V", [t_s1[c], t_c3[c]])
+            t_s2 = done("V", g.vector.tensor_tensor_scan(T.sc2[:, o2:o2 + 64], T.cmp[:, at[c] + 2 * n:at[c] + 2 * n + 64],
+                                                         T.cmp[:, at[c] + 2 * n + 64:at[c] + 2 * n + 128],
+                                                         T.sc1[:, o1:o1 + 1], OP.add, OP.add))
+        rk = T.sc2[:, 256 * b + 63:256 * b + 256:64]
+
+        F = 16 * b
+        t_n = ts([t_s2], T.fl[:, F + 8:F + 12], rk, 16.0, -16.0, OP.is_ge, OP.mult)
+        ts([], T.fl[:, F:F + 4], rk, 16.0, None, OP.is_lt)
+        t_f = ts([], T.fl[:, F + 4:F + 8], rk, 16.0, None, OP.is_ge)
+        t_rm = tt([t_n], T.fl[:, F + 12:F + 16], rk, T.fl[:, F + 8:F + 12], OP.add)
+        A = 4 * LW * b
+        tt([t_f, t_nh, t_nl, t_ab0], T.ab[:, A + 512:A + 520], T.fl[:, F:F + 8], T.nh[:], OP.mult)
+        tt([], T.ab[:, A + 520:A + 528], T.fl[:, F:F + 8], T.nl[:], OP.mult)
+        for t in range(4):
+            t_a = ts([t_rm, t_i16], T.ab[:, A + t:A + 512:4], T.i16[:], T.fl[:, F + 12 + t:F + 13 + t], None, OP.is_equal)
+        t_abq = quant([t_a], T.abq, T.abs, LW * b, LW, T.ab, A)
+        L = LW * b
+        mm([t_abq], T.psr[:, 0:128], L, T.abq, T.abs, L + 128, T.abq, T.abs, 128, True, False)
+        t_l = mm([], T.psr[:, 0:128], L, T.abq, T.abs, L + 130, T.abq, T.abs, 128, False, True)
+        t_off = cp([t_l], T.off[:, 2 * b:2 * b + 2], T.psr[:, 0:2])
+
+        m0 = 128 * b + K * rank
+        t_pk = cp([t_off], T.mq[:, m0:m0 + K].bitcast(dt.uint32),
+                  T.xq[:, 0:P].bitcast(dt.uint32).indirect(T.off[:, 2 * b:2 * b + 2]))
+        t_psc = act([t_off], T.ms[:, m0:m0 + K], T.xs[:, 0:P].indirect(T.off[:, 2 * b:2 * b + 2]), AF.Copy)
+        need("G", [t_pk])
+        send(T.mq[:, m0:m0 + K].bitcast(dt.uint8), b)
+        need("G", [t_psc])
+        send(T.ms[:, m0:m0 + K], b)
+
+        t_lst = cp([t_off], T.lst[:, 2 * b:2 * b + 2], T.off[:, 2 * b:2 * b + 2])
+        for h in range(2):
+            outs.append(dma("Y", T.ch[b:b + 1, 16 * h:16 * h + 16], T.lst[0:16, 2 * b + h:2 * b + h + 1], "dout", [t_lst]))
+        if b < R - 1:
+            t_pen = ts([t_s2], T.pen[:, 4 * b:4 * b + 4], rk, 32.0, GONE, OP.is_lt, OP.mult)
+            t_srp = tt([t_pen, t_bc], T.srp[:, 4 * b:4 * b + 4], T.bc[:, B:B + 128:32], T.pen[:, 4 * b:4 * b + 4], OP.add)
+        if b == 0:
+            for o in range(O):
+                t_wq = quant([dw], T.wq, T.ws, 128 * o, 128, T.wr, 512 * o)
+            t_st = cp([t_bc], T.st[:, 0:4], T.bc[:, 0:128:32])
+        else:
+            i = 4 * (b - 1)
+            t_q = ts([t_m], T.mq4[:, i:i + 4], T.mx[:, i:i + 4], -0.25, None, OP.mult)
+            t_st = tt([t_q, t_st], T.st[:, 4 * b:4 * b + 4], T.mq4[:, i:i + 4], T.st[:, i:i + 4], OP.add)
+        if b == R - 1:
+            for a in range(4):
+                for c in range(4):
+                    j = 128 * a + 32 * c
+                    outs.append(dma("Y", T.se[0:1, j:j + 32], T.st[32 * a:32 * a + 32, 4 * b + c:4 * b + c + 1], "dout", [t_st]))
+
+        arrived = [("arr%d" % b, (N - 1) * 2 * engs), t_pk, t_psc]
+        if b < R - 1:
+            t_mm = [mm(arrived + [free_c[c]], T.psc[:, 512 * c:512 * c + 128], 128 * c, T.pq, T.ps, 128 * b, T.mq, T.ms, 128)
+                    for c in range(4)]
+            t_red = [None] * 4
+
+            def bcast(c):
+                return ts([t_red[c], t_srp, t_quart], T.bc[:, B + 128 + 32 * c:B + 160 + 32 * c], T.quart[:],
+                          T.mx[:, 4 * b + c:4 * b + c + 1], T.srp[:, 4 * b + c:4 * b + c + 1], OP.mult, OP.add)
+            for c in range(4):
+                need("V", [t_mm[c]])
+                t_red[c] = done("V", g.vector.tensor_reduce(T.mx[:, 4 * b + c:4 * b + c + 1], T.psc[:, 512 * c:512 * c + 128],
+                                                            AxisListType.X, OP.max))
+                if c:
+                    bcast(c - 1)
+            t_bc = bcast(3)
+            free_c = t_red
+            t_m = t_red[3]
+        for o in range(O):
+            t_y = mm(arrived + [t_wq] + ([free_y[o]] if free_y[o] else []), T.psy[:, 512 * o:512 * o + 128],
+                     128 * o, T.wq, T.ws, 128 * b, T.mq, T.ms, 128)
+            c0 = P * o + 128 * b
+            if b == R - 1 and o == 0:
+                free_y[o] = cp([t_y], T.ysb[:, c0:c0 + 128], T.psy[:, 512 * o:512 * o + 128])
+            else:
+                free_y[o] = act([t_y], T.ysb[:, c0:c0 + 128], T.psy[:, 512 * o:512 * o + 128], AF.Copy)
+            e = "S" if b == R - 1 and o == 1 else "Y"
+            outs.append(dma(e, T.y[:, c0:c0 + 128], T.ysb[:, c0:c0 + 128], "dout", [free_y[o]]))
+
+    need("Y", [outs[-1]])
+    need("G", [("loc", 2 * R * engs)])
+    for s in ("sv", "ss", "sp", "sg"):
+        need("Y", [(s, count[s])])

@@ -3,12 +3,20 @@ from concourse.mybir import dt, AluOpType, AxisListType, ActivationFunctionType
 
 OP = AluOpType
 P, K, R, O, N = 512, 32, 4, 2, 4
-CW = 640
-LW = 258
+CW = 514
+LW = 132
 KAPPA = 2.0 ** -24 * (1.0 + 2.0 ** -10)
 TINY = 2.0 ** -124
 BIG = 9e29
 GONE = -1e29
+SB = (2, 3)
+SC = (3,)
+GW = 1536
+
+
+def score(rank):
+    return 2.0 * rank - 128.0
+
 
 X4 = "float8_e4m3fn_x4"
 SCRATCH = {
@@ -19,10 +27,13 @@ SCRATCH = {
     "us": ("sbuf", [128, 128], "uint8"),
     "xr": ("sbuf", [128, 4 * P], "bfloat16"),
     "xp": ("sbuf", [128, 4 * P], "bfloat16"),
+    "xe": ("sbuf", [128, 4 * P], "bfloat16"),
     "xq": ("sbuf", [128, P], X4),
     "xs": ("sbuf", [128, P], "uint8"),
     "pq": ("sbuf", [128, P], X4),
     "ps": ("sbuf", [128, P], "uint8"),
+    "eq": ("sbuf", [128, P], X4),
+    "es": ("sbuf", [128, P], "uint8"),
     "wr": ("sbuf", [128, 512 * O], "bfloat16"),
     "wq": ("sbuf", [128, 128 * O], X4),
     "ws": ("sbuf", [128, 128 * O], "uint8"),
@@ -36,15 +47,22 @@ SCRATCH = {
     "i16": ("sbuf", [128, 128], "bfloat16"),
     "w16": ("sbuf", [128, 8], "int32"),
     "wand": ("sbuf", [128, 8], "int32"),
+    "nt": ("sbuf", [128, 8], "float32"),
     "nl": ("sbuf", [128, 8], "bfloat16"),
     "nh": ("sbuf", [128, 8], "bfloat16"),
     "bc": ("sbuf", [128, 128 * R], "float32"),
+    "be": ("sbuf", [128, 128 * R], "float32"),
     "srt": ("sbuf", [128, 128 * R], "float32"),
     "srh": ("sbuf", [128, 128 * R], "float32"),
     "row": ("sbuf", [128, P * R], "float32"),
+    "rowe": ("sbuf", [128, 128 * R], "float32"),
     "dd": ("sbuf", [128, 4 * R], "float32"),
     "thr": ("sbuf", [128, 16 * R], "float32"),
     "cmp": ("sbuf", [128, CW * 4 * R], "bfloat16"),
+    "sg1": ("sbuf", [128, GW * R], "bfloat16"),
+    "sg2": ("sbuf", [128, GW * R], "bfloat16"),
+    "acc": ("sbuf", [128, 4 * R], "float32"),
+    "acc2": ("sbuf", [128, 4 * R], "float32"),
     "sc1": ("sbuf", [128, 256 * 4 * R], "bfloat16"),
     "sc2": ("sbuf", [128, 64 * 4 * R], "bfloat16"),
     "fl": ("sbuf", [128, 16 * R], "bfloat16"),
@@ -55,15 +73,19 @@ SCRATCH = {
     "lst": ("sbuf", [128, 2 * R], "float32"),
     "pen": ("sbuf", [128, 4 * R], "float32"),
     "srp": ("sbuf", [128, 4 * R], "float32"),
+    "sre": ("sbuf", [128, 4 * R], "float32"),
     "mx": ("sbuf", [128, 4 * R], "float32"),
+    "me": ("sbuf", [128, 4 * R], "float32"),
     "mq4": ("sbuf", [128, 4 * R], "float32"),
     "st": ("sbuf", [128, 4 * R], "float32"),
+    "sf": ("sbuf", [128, 32], "float32"),
+    "sft": ("sbuf", [128, 32], "float32"),
     "ysb": ("sbuf", [128, O * P], "float32"),
     "psc": ("psum", [128, 2048], "float32"),
     "psr": ("psum", [128, 1024], "float32"),
     "psy": ("psum", [128, 1024], "float32"),
 }
-SEMAPHORES = ["sv", "ss", "sp", "sg", "du", "dx0", "dx1", "dx2", "dx3", "dw", "dout",
+SEMAPHORES = ["sv", "ss", "sp", "sg", "du", "dx0", "dx1", "dx2", "dx3", "dw", "dsr", "dout",
               "arr0", "arr1", "arr2", "arr3", "loc"]
 
 
@@ -108,6 +130,18 @@ def rank_program(g, core, T, topo):
         need("V", deps)
         return done("V", g.vector.tensor_copy(out, in_))
 
+    def turn(deps, out, in_):
+        need("V", deps)
+        return done("V", g.vector.transpose(out, in_))
+
+    def scan(deps, out, d0, d1, init):
+        need("V", deps)
+        return done("V", g.vector.tensor_tensor_scan(out, d0, d1, init, OP.add, OP.add))
+
+    def rmax(deps, out, in_):
+        need("V", deps)
+        return done("V", g.vector.tensor_reduce(out, in_, AxisListType.X, OP.max))
+
     def act(deps, out, in_, func, **kw):
         need("S", deps)
         return done("S", g.scalar.activation(out, in_, func, **kw))
@@ -131,7 +165,7 @@ def rank_program(g, core, T, topo):
     dx = [None] * 4
     for a in range(4):
         dx[a] = dma("SYSY"[a], T.xr[:, 512 * a:512 * a + 512], T.x[:, 512 * a:512 * a + 512], "dx%d" % a)
-    dw = dma("Y", T.wr[:], T.w[:], "dw")
+    dw = dma("Y", T.wr[:], T.w[:], "dw", [dx[2], dx[3]])
 
     t_ones = fill(T.ones[:], 1.0)
     t_onef = fill(T.onef[:], 1.0)
@@ -147,18 +181,31 @@ def rank_program(g, core, T, topo):
         v = slice(32 * a, 32 * a + 32)
         t_mask = done("G", g.affine_select(T.mask[v, :], T.big[v, :], [[0, 4], [1, 32]], OP.is_ge, -BIG, 0, -1))
     gneed([])
-    t_i16 = done("G", g.iota(T.i16[:], [[0, 8], [1, 16]], 0, 0, allow_small_or_imprecise_dtypes=True))
+    t_i16 = done("G", g.iota(T.i16[:], [[0, 8], [2, 16]], int(score(0)), 0, allow_small_or_imprecise_dtypes=True))
+    t_sf = fill(T.sf[:], 0.0)
+    pads = [[64.0 * ((c in SB) + (c in SC and b > 0)) for c in range(4)] for b in range(R)]
     for b in range(R):
-        t_ab0 = fill(T.ab[:, 4 * LW * b + 528:4 * LW * b + 4 * LW], 0.0)
+        for c in range(4):
+            if pads[b][c]:
+                o = CW * (4 * b + c)
+                fill(T.cmp[:, o:o + 2], pads[b][c])
     t_wand = ts([t_w16], T.wand[:], T.w16[:], 31, None, OP.bitwise_and)
-    t_nl = ts([t_wand], T.nl[:], T.wand[:], 16, None, OP.subtract)
-    t_nh = tt([t_wand, t_w16], T.nh[:], T.w16[:], T.wand[:], OP.subtract)
+    t_nl = ts([t_wand], T.nl[:], T.wand[:], -16.0, -1.0 / 32, OP.add, OP.mult)
+    t_nt = tt([], T.nt[:], T.w16[:], T.wand[:], OP.subtract)
+    t_nh = ts([t_nt], T.nh[:], T.nt[:], -1.0 / 32, None, OP.mult)
 
     for t in range(4):
         t_ut = ts([du, t_ones], T.ut[:, t:512:4], T.ones[:], T.uc[:, t:t + 1], None, OP.mult)
     t_uq = quant([t_ut], T.uq, T.us, 0, 128, T.ut, 0)
 
     t_xq, t_cv, t_cs, t_row = [None] * 4, None, None, [None] * 2
+
+    def natural(a):
+        t_xq[a] = quant([dx[a]], T.xq, T.xs, 128 * a, 128, T.xr, 512 * a)
+
+    def rows(h):
+        t_row[h] = mm([t_xq[2 * h + 1], t_uq], T.psr[:, 512 * h:512 * h + 256], 0, T.uq, T.us, 256 * h, T.xq, T.xs, 256)
+
     for a in range(4):
         for c in range(4):
             out = T.xp[:, 512 * c + 128 * a:512 * c + 128 * a + 128]
@@ -167,17 +214,20 @@ def rank_program(g, core, T, topo):
                 t_cv = cp([dx[a]], out, in_)
             else:
                 t_cs = act([dx[a]], out, in_, AF.Copy)
-        t_xq[a] = quant([dx[a]], T.xq, T.xs, 128 * a, 128, T.xr, 512 * a)
-        if a % 2:
-            h = a // 2
-            t_row[h] = mm([t_xq[a], t_uq], T.psr[:, 512 * h:512 * h + 256], 0, T.uq, T.us, 256 * h, T.xq, T.xs, 256)
-    t_pq, t_col = [None] * 4, [None] * 4
+        if a < 3:
+            natural(a)
+        if a == 1:
+            rows(0)
+    t_pq, t_col, t_b4, t_srt = [None] * 4, [None] * 4, [None] * 4, None
     for c in range(4):
         t_pq[c] = quant([t_cv if c < 2 else t_cs], T.pq, T.ps, 128 * c, 128, T.xp, 512 * c)
         t_col[c] = mm([t_pq[c], t_uq], T.psc[:, 512 * c:512 * c + 128], 128 * c, T.pq, T.ps, 0, T.uq, T.us, 128)
+    natural(3)
+    rows(1)
     for c in range(4):
-        t_bc = cp([t_col[c]], T.bc[:, 32 * c:32 * c + 32], T.psc[:, 512 * c:512 * c + 32])
-    free_c = [t_bc] * 4
+        t_b4[c] = cp([t_col[c]], T.bc[:, 32 * c:32 * c + 32], T.psc[:, 512 * c:512 * c + 32])
+        t_srt = turn([], T.srt[:, 32 * c:32 * c + 32], T.psc[:, 512 * c:512 * c + 32])
+    free_c = [t_srt] * 4
 
     dests = [c for c in T.cores if c != core]
     mask = topo.mask(core, dests[0])
@@ -192,78 +242,144 @@ def rank_program(g, core, T, topo):
         g.remote_dma_fused([RemoteDMATransfer(dst_ids=ids, dma_engine_mask=mask, remote_sem=T.sem["arr%d" % b],
                                               srcs=[view], dsts=[view] * len(ids))], local_sem=T.sem.loc)
 
-    t_wq = t_st = t_m = t_srp = None
+    t_wq = t_st = t_m = t_srp = t_sre = t_eq = None
+    t_ext = [None] * 4
+    t_y = [None] * O
     free_y = [None] * O
     outs = []
+
+    def store(b, o, e):
+        c0 = P * o + 128 * b
+        out, in_ = T.ysb[:, c0:c0 + 128], T.psy[:, 512 * o:512 * o + 128]
+        free_y[o] = cp([t_y[o]], out, in_) if e == "V" else act([t_y[o]], out, in_, AF.Copy)
+        outs.append(dma("Y" if b < R - 1 or o == 0 else "S", T.y[:, c0:c0 + 128], out, "dout", [free_y[o]]))
+
     for b in range(R):
         B = 128 * b
-        need("V", [t_bc])
-        t_srt = done("V", g.vector.transpose(T.srt[:, B:B + 128], T.bc[:, B:B + 128]))
-        t_d = act([t_bc], T.dd[:, 4 * b:4 * b + 4], T.bc[:, B:B + 128:32], AF.Abs, bias=TINY, scale=KAPPA)
-        t_pb = [None] * 4
+        sc = [T.bc[:, B + 32 * c:B + 32 * c + 1] for c in range(4)]
+        at = [CW * (4 * b + c) for c in range(4)]
+        cor = [at[c] + (2 if pads[b][c] else 0) for c in range(4)]
+        rest = [cor[c] + 128 - 32 * c for c in range(4)]
+        t_d = act(t_b4, T.dd[:, 4 * b:4 * b + 4], T.bc[:, B:B + 128:32], AF.Abs, bias=TINY, scale=KAPPA)
+        for c in range(4):
+            t_thr = act([t_d, t_mg, t_b4[c]], T.thr[:, 16 * b + 4 * c:16 * b + 4 * c + 4], T.mg[:], AF.Identity, bias=sc[c],
+                        scale=T.dd[:, 4 * b + c:4 * b + c + 1])
+        thr = [[T.thr[:, 16 * b + 4 * c + a:16 * b + 4 * c + a + 1] for a in range(4)] for c in range(4)]
         if b:
-            for a in range(4):
+            t_pb = [None] * 4
+            for a in range(3):
                 gneed([t_srt])
                 t_pb[a] = done("G", g.partition_broadcast(T.row[:, P * b + 128 * a:P * b + 128 * a + 128],
                                                           T.srt[32 * a:32 * a + 1, B:B + 128], 128))
-        sc = [T.bc[:, B + 32 * c:B + 32 * c + 1] for c in range(4)]
-        at = [CW * (4 * b + c) for c in range(4)]
-        t_srh = tt([t_srt, t_mask], T.srh[:, B:B + 128], T.srt[:, B:B + 128], T.mask[:], OP.min)
-        for c in range(3):
-            ts([], T.cmp[:, at[c] + 32:at[c] + 128 - 32 * c], T.srt[:, B + 32 * c + 32:B + 128], sc[c], -1.0,
-               OP.is_equal, OP.mult)
-        for c in range(4):
-            ts([t_srh], T.cmp[:, at[c]:at[c] + 32], T.srh[:, B + 32 * c:B + 32 * c + 32], sc[c], -1.0,
-               OP.is_equal, OP.mult)
-        for c in range(4):
-            t_thr = ts([t_d, t_mg], T.thr[:, 16 * b + 4 * c:16 * b + 4 * c + 4], T.mg[:], T.dd[:, 4 * b + c:4 * b + c + 1],
-                       sc[c], OP.mult, OP.add)
-
-        def compare(a, c):
-            if b:
-                row, dep = T.row[:, P * b + 128 * a:P * b + 128 * a + 128], t_pb[a]
-            else:
-                row, dep = T.psr[:, 512 * (a // 2) + 128 * (a % 2):512 * (a // 2) + 128 * (a % 2) + 128], t_row[a // 2]
-            o = at[c] + 128 - 32 * c + 128 * a
-            i = 16 * b + 4 * c + a
-            return ts([t_thr, dep], T.cmp[:, o:o + 128], row, T.thr[:, i:i + 1], None, OP.is_ge)
-
-        for a in range(3):
+            row = [T.row[:, P * b + 128 * a:P * b + 128 * a + 128] for a in range(3)] + [T.rowe[:, B:B + 128]]
+            s2, order = 3, [3, 1, 2]
+            t_me, t_be = [None] * 4, None
             for c in range(4):
-                t_c = compare(a, c)
+                i = 4 * (b - 1) + c
+                t_me[c] = rmax([t_ext[c]], T.me[:, i:i + 1], T.psc[:, 512 * c:512 * c + 128])
+                t_be = act([t_me[c], t_sre, t_quart], T.be[:, B + 32 * c:B + 32 * c + 32], T.quart[:], AF.Identity,
+                           bias=T.sre[:, i:i + 1], scale=T.me[:, i:i + 1])
+            free_c = t_me
+        else:
+            t_pb = [t_row[a // 2] for a in range(4)]
+            row = [T.psr[:, 512 * (a // 2) + 128 * (a % 2):512 * (a // 2) + 128 * (a % 2) + 128] for a in range(4)]
+            s2, order = 1, [2, 3, 1]
+        for c in range(3):
+            ts([t_srt, t_b4[c]], T.cmp[:, cor[c] + 32:cor[c] + 128 - 32 * c], T.srt[:, B + 32 * c + 32:B + 128], sc[c], -2.0,
+               OP.is_equal, OP.mult)
+        t_srh = tt([t_mask], T.srh[:, B:B + 128], T.srt[:, B:B + 128], T.mask[:], OP.min)
+        if b:
+            t_pb[3] = turn([t_be], T.rowe[:, B:B + 128], T.be[:, B:B + 128])
+        for c in range(4):
+            t_cor = ts([t_srh], T.cmp[:, cor[c]:cor[c] + 32], T.srh[:, B + 32 * c:B + 32 * c + 32], sc[c], -2.0,
+                       OP.is_equal, OP.mult)
+        t_acc = [None] * 4
+        g1 = [GW * b + 256 * c for c in range(4)]
+        sc3 = SC if b else ()
+        t_last = {}
+        for c in range(4):
+            t_sg = act([t_pb[0], t_b4[c]], T.sg1[:, g1[c]:g1[c] + 128], row[0], AF.Sign, bias=sc[c], scale=-1.0)
+        for c in SB:
+            t_sg = act([t_pb[s2], t_thr], T.sg1[:, g1[c] + 128:g1[c] + 256], row[s2], AF.Sign, bias=thr[c][s2], scale=-1.0)
+        t_psr = t_sg
+        for c in range(4):
+            w = 256 if c in SB else 128
+            t_acc[c] = act([t_sg], T.sg2[:, g1[c]:g1[c] + w], T.sg1[:, g1[c]:g1[c] + w], AF.Sign, bias=0.5, scale=-1.0,
+                           accum_out=T.acc[:, 4 * b + c:4 * b + c + 1])
+        g3 = GW * b + 1024
+        for k in range(len(sc3)):
+            t_sg = act([t_pb[2], t_thr], T.sg1[:, g3 + 128 * k:g3 + 128 * k + 128], row[2], AF.Sign, bias=thr[sc3[k]][2],
+                       scale=-1.0)
+        for k in range(len(sc3)):
+            c = sc3[k]
+            t_last[c] = act([t_sg], T.sg2[:, g3 + 128 * k:g3 + 128 * k + 128], T.sg1[:, g3 + 128 * k:g3 + 128 * k + 128],
+                            AF.Sign, bias=0.5, scale=-1.0, accum_out=T.acc2[:, 4 * b + c:4 * b + c + 1])
+        if b:
+            for o in range(O):
+                store(b - 1, o, "S")
+
+        used = [0] * 4
+        t_c = [None] * 4
+
+        def compare(a):
+            for c in range(4):
+                if (a == s2 and c in SB) or (a == order[2] and c in sc3):
+                    continue
+                o = rest[c] + 128 * used[c]
+                used[c] += 1
+                t_c[c] = ts([t_thr, t_pb[a]] + ([t_psr] if b == 0 and a == 1 else []), T.cmp[:, o:o + 128], row[a],
+                            thr[c][a], 2.0, OP.is_ge, OP.mult)
+
         t_s1 = [None] * 4
-        need("V", [t_c])
-        for c in range(4):
-            n = 256 - 16 * c
+        e1, e2 = [0] * 4, [0] * 4
+
+        def first(c, chunks):
+            n = (rest[c] + 128 * chunks - at[c]) // 2
             o1 = 256 * (4 * b + c)
-            t_s1[c] = done("V", g.vector.tensor_tensor_scan(T.sc1[:, o1:o1 + n], T.cmp[:, at[c]:at[c] + n],
-                                                            T.cmp[:, at[c] + n:at[c] + 2 * n], 0.0, OP.add, OP.add))
-        t_c3 = [compare(3, c) for c in range(4)]
+            e1[c], e2[c] = o1 + n - 1, at[c] + 2 * n
+            t_s1[c] = scan([t_c[c], t_acc[c], t_cor], T.sc1[:, o1:o1 + n], T.cmp[:, at[c]:at[c] + n],
+                           T.cmp[:, at[c] + n:at[c] + 2 * n], T.acc[:, 4 * b + c:4 * b + c + 1])
+
+        compare(order[0])
+        compare(order[1])
+        early = list(used)
+        if b:
+            for c in range(4):
+                if c not in SB:
+                    first(c, early[c])
+        compare(order[2])
         for c in range(4):
-            n = 256 - 16 * c
-            o1 = 256 * (4 * b + c) + n - 1
+            if t_s1[c] is None:
+                first(c, early[c] if b else used[c] - 1)
+        for c in range(4):
             o2 = 64 * (4 * b + c)
-            need("V", [t_s1[c], t_c3[c]])
-            t_s2 = done("V", g.vector.tensor_tensor_scan(T.sc2[:, o2:o2 + 64], T.cmp[:, at[c] + 2 * n:at[c] + 2 * n + 64],
-                                                         T.cmp[:, at[c] + 2 * n + 64:at[c] + 2 * n + 128],
-                                                         T.sc1[:, o1:o1 + 1], OP.add, OP.add))
+            e = e2[c]
+            if c in sc3:
+                t_s2 = tt([t_s1[c], t_last[c]], T.sc2[:, o2 + 63:o2 + 64], T.sc1[:, e1[c]:e1[c] + 1],
+                          T.acc2[:, 4 * b + c:4 * b + c + 1], OP.add)
+            else:
+                t_s2 = scan([t_s1[c], t_c[c]], T.sc2[:, o2:o2 + 64], T.cmp[:, e:e + 64], T.cmp[:, e + 64:e + 128],
+                            T.sc1[:, e1[c]:e1[c] + 1])
         rk = T.sc2[:, 256 * b + 63:256 * b + 256:64]
 
         F = 16 * b
-        t_n = ts([t_s2], T.fl[:, F + 8:F + 12], rk, 16.0, -16.0, OP.is_ge, OP.mult)
-        ts([], T.fl[:, F:F + 4], rk, 16.0, None, OP.is_lt)
-        t_f = ts([], T.fl[:, F + 4:F + 8], rk, 16.0, None, OP.is_ge)
-        t_rm = tt([t_n], T.fl[:, F + 12:F + 16], rk, T.fl[:, F + 8:F + 12], OP.add)
+        t_n = ts([t_s2], T.fl[:, F + 4:F + 8], rk, score(16), -32.0, OP.is_ge, OP.mult)
+        t_f = ts([], T.fl[:, F:F + 4], rk, score(16), -32.0, OP.is_lt, OP.mult)
+        if b < R - 1:
+            t_pen = ts([], T.pen[:, 4 * b:4 * b + 4], rk, score(32), GONE, OP.is_lt, OP.mult)
+        t_rm = tt([t_n], T.fl[:, F + 12:F + 16], rk, T.fl[:, F + 4:F + 8], OP.add)
         A = 4 * LW * b
-        tt([t_f, t_nh, t_nl, t_ab0], T.ab[:, A + 512:A + 520], T.fl[:, F:F + 8], T.nh[:], OP.mult)
+        tt([t_f, t_nh, t_nl], T.ab[:, A + 512:A + 520], T.fl[:, F:F + 8], T.nh[:], OP.mult)
         tt([], T.ab[:, A + 520:A + 528], T.fl[:, F:F + 8], T.nl[:], OP.mult)
         for t in range(4):
             t_a = ts([t_rm, t_i16], T.ab[:, A + t:A + 512:4], T.i16[:], T.fl[:, F + 12 + t:F + 13 + t], None, OP.is_equal)
+        if b < R - 1:
+            t_srp = tt([t_pen, t_b4[3]], T.srp[:, 4 * b:4 * b + 4], T.bc[:, B:B + 128:32], T.pen[:, 4 * b:4 * b + 4], OP.add)
         t_abq = quant([t_a], T.abq, T.abs, LW * b, LW, T.ab, A)
         L = LW * b
-        mm([t_abq], T.psr[:, 0:128], L, T.abq, T.abs, L + 128, T.abq, T.abs, 128, True, False)
-        t_l = mm([], T.psr[:, 0:128], L, T.abq, T.abs, L + 130, T.abq, T.abs, 128, False, True)
-        t_off = cp([t_l], T.off[:, 2 * b:2 * b + 2], T.psr[:, 0:2])
+        mm([t_abq], T.psr[:, 0:128], L, T.abq, T.abs, L + 2, T.abq, T.abs, 128, True, False)
+        t_l = mm([], T.psr[:, 0:128], L, T.abq, T.abs, L + 4, T.abq, T.abs, 128, False, True)
+        t_off = cp([t_l], T.off[:, 2 * b:2 * b + 2], T.psr[:, 126:128])
 
         m0 = 128 * b + K * rank
         t_pk = cp([t_off], T.mq[:, m0:m0 + K].bitcast(dt.uint32),
@@ -275,53 +391,58 @@ def rank_program(g, core, T, topo):
         send(T.ms[:, m0:m0 + K], b)
 
         t_lst = cp([t_off], T.lst[:, 2 * b:2 * b + 2], T.off[:, 2 * b:2 * b + 2])
+        if b < R - 1:
+            for a in range(4):
+                t_sre = dma("Y", T.sre[32 * a:32 * a + 32, 4 * b:4 * b + 4], T.srp[96:128, 4 * b:4 * b + 4], "dsr", [t_srp])
         for h in range(2):
             outs.append(dma("Y", T.ch[b:b + 1, 16 * h:16 * h + 16], T.lst[0:16, 2 * b + h:2 * b + h + 1], "dout", [t_lst]))
-        if b < R - 1:
-            t_pen = ts([t_s2], T.pen[:, 4 * b:4 * b + 4], rk, 32.0, GONE, OP.is_lt, OP.mult)
-            t_srp = tt([t_pen, t_bc], T.srp[:, 4 * b:4 * b + 4], T.bc[:, B:B + 128:32], T.pen[:, 4 * b:4 * b + 4], OP.add)
         if b == 0:
+            t_st = cp([t_b4[3]], T.st[:, 0:4], T.bc[:, 0:128:32])
+            for c in range(4):
+                for k in range(4):
+                    t_xe = cp([dx[3]], T.xe[:, 512 * c + 128 * k:512 * c + 128 * k + 128],
+                              T.xr[:, 1536 + 128 * c:1536 + 128 * c + 128])
             for o in range(O):
                 t_wq = quant([dw], T.wq, T.ws, 128 * o, 128, T.wr, 512 * o)
-            t_st = cp([t_bc], T.st[:, 0:4], T.bc[:, 0:128:32])
+            for c in range(4):
+                t_eq = quant([t_xe], T.eq, T.es, 128 * c, 128, T.xe, 512 * c)
         else:
             i = 4 * (b - 1)
             t_q = ts([t_m], T.mq4[:, i:i + 4], T.mx[:, i:i + 4], -0.25, None, OP.mult)
-            t_st = tt([t_q, t_st], T.st[:, 4 * b:4 * b + 4], T.mq4[:, i:i + 4], T.st[:, i:i + 4], OP.add)
-        if b == R - 1:
-            for a in range(4):
-                for c in range(4):
-                    j = 128 * a + 32 * c
-                    outs.append(dma("Y", T.se[0:1, j:j + 32], T.st[32 * a:32 * a + 32, 4 * b + c:4 * b + c + 1], "dout", [t_st]))
+            if b < R - 1:
+                t_st = tt([t_q, t_st], T.st[:, 4 * b:4 * b + 4], T.mq4[:, i:i + 4], T.st[:, i:i + 4], OP.add)
+            else:
+                t_st = tt([t_q, t_st, t_sf], T.sf[:, 0:4], T.mq4[:, i:i + 4], T.st[:, i:i + 4], OP.add)
+                t_sft = turn([t_st], T.sft[:], T.sf[:])
+                for a in range(4):
+                    outs.append(dma("Y", T.se[0:1, 128 * a:128 * a + 128], T.sft[32 * a:32 * a + 4, :], "dout", [t_sft]))
 
         arrived = [("arr%d" % b, (N - 1) * 2 * engs), t_pk, t_psc]
         if b < R - 1:
             t_mm = [mm(arrived + [free_c[c]], T.psc[:, 512 * c:512 * c + 128], 128 * c, T.pq, T.ps, 128 * b, T.mq, T.ms, 128)
                     for c in range(4)]
             t_red = [None] * 4
-
-            def bcast(c):
-                return ts([t_red[c], t_srp, t_quart], T.bc[:, B + 128 + 32 * c:B + 160 + 32 * c], T.quart[:],
-                          T.mx[:, 4 * b + c:4 * b + c + 1], T.srp[:, 4 * b + c:4 * b + c + 1], OP.mult, OP.add)
+            nb = B + 128
+            t_b4 = [None] * 4
             for c in range(4):
-                need("V", [t_mm[c]])
-                t_red[c] = done("V", g.vector.tensor_reduce(T.mx[:, 4 * b + c:4 * b + c + 1], T.psc[:, 512 * c:512 * c + 128],
-                                                            AxisListType.X, OP.max))
-                if c:
-                    bcast(c - 1)
-            t_bc = bcast(3)
-            free_c = t_red
+                i = 4 * b + c
+                m1, s1, out = T.mx[:, i:i + 1], T.srp[:, i:i + 1], T.bc[:, nb + 32 * c:nb + 32 * c + 32]
+                t_red[c] = rmax([t_mm[c]], m1, T.psc[:, 512 * c:512 * c + 128])
+                if c < 3:
+                    t_b4[c] = act([t_red[c], t_srp, t_quart], out, T.quart[:], AF.Identity, bias=s1, scale=m1)
+                else:
+                    t_b4[c] = ts([t_red[c]], out, T.quart[:], m1, s1, OP.mult, OP.add)
+            turn([t_b4[2]], T.srt[:, nb:nb + 96], T.bc[:, nb:nb + 96])
+            t_srt = turn([t_b4[3]], T.srt[:, nb + 96:nb + 128], T.bc[:, nb + 96:nb + 128])
             t_m = t_red[3]
+            t_ext = [mm([t_red[c], t_eq], T.psc[:, 512 * c:512 * c + 128], 128 * c, T.eq, T.es, 128 * b, T.mq, T.ms, 128)
+                     for c in range(4)]
         for o in range(O):
-            t_y = mm(arrived + [t_wq] + ([free_y[o]] if free_y[o] else []), T.psy[:, 512 * o:512 * o + 128],
-                     128 * o, T.wq, T.ws, 128 * b, T.mq, T.ms, 128)
-            c0 = P * o + 128 * b
-            if b == R - 1 and o == 0:
-                free_y[o] = cp([t_y], T.ysb[:, c0:c0 + 128], T.psy[:, 512 * o:512 * o + 128])
-            else:
-                free_y[o] = act([t_y], T.ysb[:, c0:c0 + 128], T.psy[:, 512 * o:512 * o + 128], AF.Copy)
-            e = "S" if b == R - 1 and o == 1 else "Y"
-            outs.append(dma(e, T.y[:, c0:c0 + 128], T.ysb[:, c0:c0 + 128], "dout", [free_y[o]]))
+            t_y[o] = mm(arrived + [t_wq] + ([free_y[o]] if free_y[o] else []), T.psy[:, 512 * o:512 * o + 128],
+                        128 * o, T.wq, T.ws, 128 * b, T.mq, T.ms, 128)
+        if b == R - 1:
+            store(b, 0, "V")
+            store(b, 1, "S")
 
     need("Y", [outs[-1]])
     need("G", [("loc", 2 * R * engs)])

from concourse.bass import DstId, RemoteDMATransfer
from concourse.mybir import dt, AluOpType, AxisListType, ActivationFunctionType

OP = AluOpType
P, K, R, O, N = 512, 32, 4, 2, 4
CW = 514
LW = 132
KAPPA = 2.0 ** -24 * (1.0 + 2.0 ** -10)
TINY = 2.0 ** -124
BIG = 9e29
GONE = -1e29
SB = (2, 3)
SC = (3,)
GW = 1536


def score(rank):
    return 2.0 * rank - 128.0


X4 = "float8_e4m3fn_x4"
SCRATCH = {
    "uc": ("sbuf", [128, 4], "bfloat16"),
    "ones": ("sbuf", [128, 128], "bfloat16"),
    "ut": ("sbuf", [128, 512], "bfloat16"),
    "uq": ("sbuf", [128, 128], X4),
    "us": ("sbuf", [128, 128], "uint8"),
    "xr": ("sbuf", [128, 4 * P], "bfloat16"),
    "xp": ("sbuf", [128, 4 * P], "bfloat16"),
    "xe": ("sbuf", [128, 4 * P], "bfloat16"),
    "xq": ("sbuf", [128, P], X4),
    "xs": ("sbuf", [128, P], "uint8"),
    "pq": ("sbuf", [128, P], X4),
    "ps": ("sbuf", [128, P], "uint8"),
    "eq": ("sbuf", [128, P], X4),
    "es": ("sbuf", [128, P], "uint8"),
    "wr": ("sbuf", [128, 512 * O], "bfloat16"),
    "wq": ("sbuf", [128, 128 * O], X4),
    "ws": ("sbuf", [128, 128 * O], "uint8"),
    "mq": ("sbuf", [128, 128 * R], X4),
    "ms": ("sbuf", [128, 128 * R], "uint8"),
    "onef": ("sbuf", [128, 4], "float32"),
    "big": ("sbuf", [128, 128], "float32"),
    "mask": ("sbuf", [128, 128], "float32"),
    "mg": ("sbuf", [128, 4], "float32"),
    "quart": ("sbuf", [128, 32], "float32"),
    "i16": ("sbuf", [128, 128], "bfloat16"),
    "w16": ("sbuf", [128, 8], "int32"),
    "wand": ("sbuf", [128, 8], "int32"),
    "nt": ("sbuf", [128, 8], "float32"),
    "nl": ("sbuf", [128, 8], "bfloat16"),
    "nh": ("sbuf", [128, 8], "bfloat16"),
    "bc": ("sbuf", [128, 128 * R], "float32"),
    "be": ("sbuf", [128, 128 * R], "float32"),
    "srt": ("sbuf", [128, 128 * R], "float32"),
    "srh": ("sbuf", [128, 128 * R], "float32"),
    "row": ("sbuf", [128, P * R], "float32"),
    "rowe": ("sbuf", [128, 128 * R], "float32"),
    "dd": ("sbuf", [128, 4 * R], "float32"),
    "thr": ("sbuf", [128, 16 * R], "float32"),
    "cmp": ("sbuf", [128, CW * 4 * R], "bfloat16"),
    "sg1": ("sbuf", [128, GW * R], "bfloat16"),
    "sg2": ("sbuf", [128, GW * R], "bfloat16"),
    "acc": ("sbuf", [128, 4 * R], "float32"),
    "acc2": ("sbuf", [128, 4 * R], "float32"),
    "sc1": ("sbuf", [128, 256 * 4 * R], "bfloat16"),
    "sc2": ("sbuf", [128, 64 * 4 * R], "bfloat16"),
    "fl": ("sbuf", [128, 16 * R], "bfloat16"),
    "ab": ("sbuf", [128, 4 * LW * R], "bfloat16"),
    "abq": ("sbuf", [128, LW * R], X4),
    "abs": ("sbuf", [128, LW * R], "uint8"),
    "off": ("sbuf", [128, 2 * R], "uint16"),
    "lst": ("sbuf", [128, 2 * R], "float32"),
    "pen": ("sbuf", [128, 4 * R], "float32"),
    "srp": ("sbuf", [128, 4 * R], "float32"),
    "sre": ("sbuf", [128, 4 * R], "float32"),
    "mx": ("sbuf", [128, 4 * R], "float32"),
    "me": ("sbuf", [128, 4 * R], "float32"),
    "mq4": ("sbuf", [128, 4 * R], "float32"),
    "st": ("sbuf", [128, 4 * R], "float32"),
    "sf": ("sbuf", [128, 32], "float32"),
    "sft": ("sbuf", [128, 32], "float32"),
    "ysb": ("sbuf", [128, O * P], "float32"),
    "psc": ("psum", [128, 2048], "float32"),
    "psr": ("psum", [128, 1024], "float32"),
    "psy": ("psum", [128, 1024], "float32"),
}
SEMAPHORES = ["sv", "ss", "sp", "sg", "du", "dx0", "dx1", "dx2", "dx3", "dw", "dsr", "dout",
              "arr0", "arr1", "arr2", "arr3", "loc"]


def rank_program(g, core, T, topo):
    rank = T.rank_of(core)
    if rank is None:
        return
    AF = ActivationFunctionType
    queue = {"V": g.vector, "S": g.scalar, "P": g.tensor, "G": g, "Y": g.sync}
    own = {"V": "sv", "S": "ss", "P": "sp", "G": "sg"}
    count, seen = {}, {}

    def need(e, deps):
        for s, v in deps:
            if seen.get((e, s), 0) < v:
                queue[e].wait_ge(T.sem[s], v)
                seen[(e, s)] = v

    def done(e, ins):
        s = own[e]
        count[s] = count.get(s, 0) + 1
        ins.then_inc(T.sem[s], 1)
        return (s, count[s])

    def dma(e, out, in_, sem, deps=()):
        need(e, deps)
        count[sem] = count.get(sem, 0) + 16
        queue[e].dma_start(out, in_).then_inc(T.sem[sem], 16)
        return (sem, count[sem])

    def ts(deps, out, in0, s1, s2, op0, op1=None):
        need("V", deps)
        if op1 is None:
            return done("V", g.vector.tensor_scalar(out, in0, s1, s2, op0))
        return done("V", g.vector.tensor_scalar(out, in0, s1, s2, op0, op1))

    def tt(deps, out, in0, in1, op):
        need("V", deps)
        return done("V", g.vector.tensor_tensor(out, in0, in1, op))

    def cp(deps, out, in_):
        need("V", deps)
        return done("V", g.vector.tensor_copy(out, in_))

    def turn(deps, out, in_):
        need("V", deps)
        return done("V", g.vector.transpose(out, in_))

    def scan(deps, out, d0, d1, init):
        need("V", deps)
        return done("V", g.vector.tensor_tensor_scan(out, d0, d1, init, OP.add, OP.add))

    def rmax(deps, out, in_):
        need("V", deps)
        return done("V", g.vector.tensor_reduce(out, in_, AxisListType.X, OP.max))

    def act(deps, out, in_, func, **kw):
        need("S", deps)
        return done("S", g.scalar.activation(out, in_, func, **kw))

    def gneed(deps):
        need("G", list(deps) + ([("sg", count["sg"])] if "sg" in count else []))

    def fill(ap, v):
        return done("V", g.vector.memset(ap, v))

    def quant(deps, q, s, a, n, src, sa):
        need("V", deps)
        return done("V", g.vector.quantize_mx(q[:, a:a + n], s[:, a:a + n], src[:, sa:sa + 4 * n]))

    def mm(deps, out, l, lq, ls, r, rq, rs, n, start=True, stop=True):
        need("P", deps)
        return done("P", g.tensor.matmul_mx(out, lq[:, l:l + 128], ls[:, l:l + 128],
                                            rq[:, r:r + n], rs[:, r:r + n], start, stop))

    du = dma("Y", T.uc[:], T.u[:, 0:4], "du")
    dx = [None] * 4
    for a in range(4):
        dx[a] = dma("SYSY"[a], T.xr[:, 512 * a:512 * a + 512], T.x[:, 512 * a:512 * a + 512], "dx%d" % a)
    dw = dma("Y", T.wr[:], T.w[:], "dw", [dx[2], dx[3]])

    t_ones = fill(T.ones[:], 1.0)
    t_onef = fill(T.onef[:], 1.0)
    t_big = fill(T.big[:], BIG)
    t_quart = fill(T.quart[:], -0.25)
    for a in range(4):
        gneed([])
        t_w16 = done("G", g.iota(T.w16[32 * a:32 * a + 32, :], [[0, 2], [32, 4]], 128 * a + 16, 1))
    gneed([t_onef])
    t_mg = done("G", g.affine_select(T.mg[:], T.onef[:], [[32, 4]], OP.is_gt, 0.0, 0, -1))
    for a in range(4):
        gneed([t_big])
        v = slice(32 * a, 32 * a + 32)
        t_mask = done("G", g.affine_select(T.mask[v, :], T.big[v, :], [[0, 4], [1, 32]], OP.is_ge, -BIG, 0, -1))
    gneed([])
    t_i16 = done("G", g.iota(T.i16[:], [[0, 8], [2, 16]], int(score(0)), 0, allow_small_or_imprecise_dtypes=True))
    t_sf = fill(T.sf[:], 0.0)
    pads = [[64.0 * ((c in SB) + (c in SC and b > 0)) for c in range(4)] for b in range(R)]
    for b in range(R):
        for c in range(4):
            if pads[b][c]:
                o = CW * (4 * b + c)
                fill(T.cmp[:, o:o + 2], pads[b][c])
    t_wand = ts([t_w16], T.wand[:], T.w16[:], 31, None, OP.bitwise_and)
    t_nl = ts([t_wand], T.nl[:], T.wand[:], -16.0, -1.0 / 32, OP.add, OP.mult)
    t_nt = tt([], T.nt[:], T.w16[:], T.wand[:], OP.subtract)
    t_nh = ts([t_nt], T.nh[:], T.nt[:], -1.0 / 32, None, OP.mult)

    for t in range(4):
        t_ut = ts([du, t_ones], T.ut[:, t:512:4], T.ones[:], T.uc[:, t:t + 1], None, OP.mult)
    t_uq = quant([t_ut], T.uq, T.us, 0, 128, T.ut, 0)

    t_xq, t_cv, t_cs, t_row = [None] * 4, None, None, [None] * 2

    def natural(a):
        t_xq[a] = quant([dx[a]], T.xq, T.xs, 128 * a, 128, T.xr, 512 * a)

    def rows(h):
        t_row[h] = mm([t_xq[2 * h + 1], t_uq], T.psr[:, 512 * h:512 * h + 256], 0, T.uq, T.us, 256 * h, T.xq, T.xs, 256)

    for a in range(4):
        for c in range(4):
            out = T.xp[:, 512 * c + 128 * a:512 * c + 128 * a + 128]
            in_ = T.xr[:, 512 * a + 128 * c:512 * a + 128 * c + 128]
            if c < 2:
                t_cv = cp([dx[a]], out, in_)
            else:
                t_cs = act([dx[a]], out, in_, AF.Copy)
        if a < 3:
            natural(a)
        if a == 1:
            rows(0)
    t_pq, t_col, t_b4, t_srt = [None] * 4, [None] * 4, [None] * 4, None
    for c in range(4):
        t_pq[c] = quant([t_cv if c < 2 else t_cs], T.pq, T.ps, 128 * c, 128, T.xp, 512 * c)
        t_col[c] = mm([t_pq[c], t_uq], T.psc[:, 512 * c:512 * c + 128], 128 * c, T.pq, T.ps, 0, T.uq, T.us, 128)
    natural(3)
    rows(1)
    for c in range(4):
        t_b4[c] = cp([t_col[c]], T.bc[:, 32 * c:32 * c + 32], T.psc[:, 512 * c:512 * c + 32])
        t_srt = turn([], T.srt[:, 32 * c:32 * c + 32], T.psc[:, 512 * c:512 * c + 32])
    free_c = [t_srt] * 4

    dests = [c for c in T.cores if c != core]
    mask = topo.mask(core, dests[0])
    ids = []
    for c in dests:
        mask &= topo.mask(core, c)
        rid, pid, _ = topo.addr(c)
        ids.append(DstId(rid=rid, pnc=pid))
    engs = bin(mask).count("1")

    def send(view, b):
        g.remote_dma_fused([RemoteDMATransfer(dst_ids=ids, dma_engine_mask=mask, remote_sem=T.sem["arr%d" % b],
                                              srcs=[view], dsts=[view] * len(ids))], local_sem=T.sem.loc)

    t_wq = t_st = t_m = t_srp = t_sre = t_eq = None
    t_ext = [None] * 4
    t_y = [None] * O
    free_y = [None] * O
    outs = []

    def store(b, o, e):
        c0 = P * o + 128 * b
        out, in_ = T.ysb[:, c0:c0 + 128], T.psy[:, 512 * o:512 * o + 128]
        free_y[o] = cp([t_y[o]], out, in_) if e == "V" else act([t_y[o]], out, in_, AF.Copy)
        outs.append(dma("Y" if b < R - 1 or o == 0 else "S", T.y[:, c0:c0 + 128], out, "dout", [free_y[o]]))

    for b in range(R):
        B = 128 * b
        sc = [T.bc[:, B + 32 * c:B + 32 * c + 1] for c in range(4)]
        at = [CW * (4 * b + c) for c in range(4)]
        cor = [at[c] + (2 if pads[b][c] else 0) for c in range(4)]
        rest = [cor[c] + 128 - 32 * c for c in range(4)]
        t_d = act(t_b4, T.dd[:, 4 * b:4 * b + 4], T.bc[:, B:B + 128:32], AF.Abs, bias=TINY, scale=KAPPA)
        for c in range(4):
            t_thr = act([t_d, t_mg, t_b4[c]], T.thr[:, 16 * b + 4 * c:16 * b + 4 * c + 4], T.mg[:], AF.Identity, bias=sc[c],
                        scale=T.dd[:, 4 * b + c:4 * b + c + 1])
        thr = [[T.thr[:, 16 * b + 4 * c + a:16 * b + 4 * c + a + 1] for a in range(4)] for c in range(4)]
        if b:
            t_pb = [None] * 4
            for a in range(3):
                gneed([t_srt])
                t_pb[a] = done("G", g.partition_broadcast(T.row[:, P * b + 128 * a:P * b + 128 * a + 128],
                                                          T.srt[32 * a:32 * a + 1, B:B + 128], 128))
            row = [T.row[:, P * b + 128 * a:P * b + 128 * a + 128] for a in range(3)] + [T.rowe[:, B:B + 128]]
            s2, order = 3, [3, 1, 2]
            t_me, t_be = [None] * 4, None
            for c in range(4):
                i = 4 * (b - 1) + c
                t_me[c] = rmax([t_ext[c]], T.me[:, i:i + 1], T.psc[:, 512 * c:512 * c + 128])
                t_be = act([t_me[c], t_sre, t_quart], T.be[:, B + 32 * c:B + 32 * c + 32], T.quart[:], AF.Identity,
                           bias=T.sre[:, i:i + 1], scale=T.me[:, i:i + 1])
            free_c = t_me
        else:
            t_pb = [t_row[a // 2] for a in range(4)]
            row = [T.psr[:, 512 * (a // 2) + 128 * (a % 2):512 * (a // 2) + 128 * (a % 2) + 128] for a in range(4)]
            s2, order = 1, [2, 3, 1]
        for c in range(3):
            ts([t_srt, t_b4[c]], T.cmp[:, cor[c] + 32:cor[c] + 128 - 32 * c], T.srt[:, B + 32 * c + 32:B + 128], sc[c], -2.0,
               OP.is_equal, OP.mult)
        t_srh = tt([t_mask], T.srh[:, B:B + 128], T.srt[:, B:B + 128], T.mask[:], OP.min)
        if b:
            t_pb[3] = turn([t_be], T.rowe[:, B:B + 128], T.be[:, B:B + 128])
        for c in range(4):
            t_cor = ts([t_srh], T.cmp[:, cor[c]:cor[c] + 32], T.srh[:, B + 32 * c:B + 32 * c + 32], sc[c], -2.0,
                       OP.is_equal, OP.mult)
        t_acc = [None] * 4
        g1 = [GW * b + 256 * c for c in range(4)]
        sc3 = SC if b else ()
        t_last = {}
        for c in range(4):
            t_sg = act([t_pb[0], t_b4[c]], T.sg1[:, g1[c]:g1[c] + 128], row[0], AF.Sign, bias=sc[c], scale=-1.0)
        for c in SB:
            t_sg = act([t_pb[s2], t_thr], T.sg1[:, g1[c] + 128:g1[c] + 256], row[s2], AF.Sign, bias=thr[c][s2], scale=-1.0)
        t_psr = t_sg
        for c in range(4):
            w = 256 if c in SB else 128
            t_acc[c] = act([t_sg], T.sg2[:, g1[c]:g1[c] + w], T.sg1[:, g1[c]:g1[c] + w], AF.Sign, bias=0.5, scale=-1.0,
                           accum_out=T.acc[:, 4 * b + c:4 * b + c + 1])
        g3 = GW * b + 1024
        for k in range(len(sc3)):
            t_sg = act([t_pb[2], t_thr], T.sg1[:, g3 + 128 * k:g3 + 128 * k + 128], row[2], AF.Sign, bias=thr[sc3[k]][2],
                       scale=-1.0)
        for k in range(len(sc3)):
            c = sc3[k]
            t_last[c] = act([t_sg], T.sg2[:, g3 + 128 * k:g3 + 128 * k + 128], T.sg1[:, g3 + 128 * k:g3 + 128 * k + 128],
                            AF.Sign, bias=0.5, scale=-1.0, accum_out=T.acc2[:, 4 * b + c:4 * b + c + 1])
        if b:
            for o in range(O):
                store(b - 1, o, "S")

        used = [0] * 4
        t_c = [None] * 4

        def compare(a):
            for c in range(4):
                if (a == s2 and c in SB) or (a == order[2] and c in sc3):
                    continue
                o = rest[c] + 128 * used[c]
                used[c] += 1
                t_c[c] = ts([t_thr, t_pb[a]] + ([t_psr] if b == 0 and a == 1 else []), T.cmp[:, o:o + 128], row[a],
                            thr[c][a], 2.0, OP.is_ge, OP.mult)

        t_s1 = [None] * 4
        e1, e2 = [0] * 4, [0] * 4

        def first(c, chunks):
            n = (rest[c] + 128 * chunks - at[c]) // 2
            o1 = 256 * (4 * b + c)
            e1[c], e2[c] = o1 + n - 1, at[c] + 2 * n
            t_s1[c] = scan([t_c[c], t_acc[c], t_cor], T.sc1[:, o1:o1 + n], T.cmp[:, at[c]:at[c] + n],
                           T.cmp[:, at[c] + n:at[c] + 2 * n], T.acc[:, 4 * b + c:4 * b + c + 1])

        compare(order[0])
        compare(order[1])
        early = list(used)
        if b:
            for c in range(4):
                if c not in SB:
                    first(c, early[c])
        compare(order[2])
        for c in range(4):
            if t_s1[c] is None:
                first(c, early[c] if b else used[c] - 1)
        for c in range(4):
            o2 = 64 * (4 * b + c)
            e = e2[c]
            if c in sc3:
                t_s2 = tt([t_s1[c], t_last[c]], T.sc2[:, o2 + 63:o2 + 64], T.sc1[:, e1[c]:e1[c] + 1],
                          T.acc2[:, 4 * b + c:4 * b + c + 1], OP.add)
            else:
                t_s2 = scan([t_s1[c], t_c[c]], T.sc2[:, o2:o2 + 64], T.cmp[:, e:e + 64], T.cmp[:, e + 64:e + 128],
                            T.sc1[:, e1[c]:e1[c] + 1])
        rk = T.sc2[:, 256 * b + 63:256 * b + 256:64]

        F = 16 * b
        t_n = ts([t_s2], T.fl[:, F + 4:F + 8], rk, score(16), -32.0, OP.is_ge, OP.mult)
        t_f = ts([], T.fl[:, F:F + 4], rk, score(16), -32.0, OP.is_lt, OP.mult)
        if b < R - 1:
            t_pen = ts([], T.pen[:, 4 * b:4 * b + 4], rk, score(32), GONE, OP.is_lt, OP.mult)
        t_rm = tt([t_n], T.fl[:, F + 12:F + 16], rk, T.fl[:, F + 4:F + 8], OP.add)
        A = 4 * LW * b
        tt([t_f, t_nh, t_nl], T.ab[:, A + 512:A + 520], T.fl[:, F:F + 8], T.nh[:], OP.mult)
        tt([], T.ab[:, A + 520:A + 528], T.fl[:, F:F + 8], T.nl[:], OP.mult)
        for t in range(4):
            t_a = ts([t_rm, t_i16], T.ab[:, A + t:A + 512:4], T.i16[:], T.fl[:, F + 12 + t:F + 13 + t], None, OP.is_equal)
        if b < R - 1:
            t_srp = tt([t_pen, t_b4[3]], T.srp[:, 4 * b:4 * b + 4], T.bc[:, B:B + 128:32], T.pen[:, 4 * b:4 * b + 4], OP.add)
        t_abq = quant([t_a], T.abq, T.abs, LW * b, LW, T.ab, A)
        L = LW * b
        mm([t_abq], T.psr[:, 0:128], L, T.abq, T.abs, L + 2, T.abq, T.abs, 128, True, False)
        t_l = mm([], T.psr[:, 0:128], L, T.abq, T.abs, L + 4, T.abq, T.abs, 128, False, True)
        t_off = cp([t_l], T.off[:, 2 * b:2 * b + 2], T.psr[:, 126:128])

        m0 = 128 * b + K * rank
        t_pk = cp([t_off], T.mq[:, m0:m0 + K].bitcast(dt.uint32),
                  T.xq[:, 0:P].bitcast(dt.uint32).indirect(T.off[:, 2 * b:2 * b + 2]))
        t_psc = act([t_off], T.ms[:, m0:m0 + K], T.xs[:, 0:P].indirect(T.off[:, 2 * b:2 * b + 2]), AF.Copy)
        need("G", [t_pk])
        send(T.mq[:, m0:m0 + K].bitcast(dt.uint8), b)
        need("G", [t_psc])
        send(T.ms[:, m0:m0 + K], b)

        t_lst = cp([t_off], T.lst[:, 2 * b:2 * b + 2], T.off[:, 2 * b:2 * b + 2])
        if b < R - 1:
            for a in range(4):
                t_sre = dma("Y", T.sre[32 * a:32 * a + 32, 4 * b:4 * b + 4], T.srp[96:128, 4 * b:4 * b + 4], "dsr", [t_srp])
        for h in range(2):
            outs.append(dma("Y", T.ch[b:b + 1, 16 * h:16 * h + 16], T.lst[0:16, 2 * b + h:2 * b + h + 1], "dout", [t_lst]))
        if b == 0:
            t_st = cp([t_b4[3]], T.st[:, 0:4], T.bc[:, 0:128:32])
            for c in range(4):
                for k in range(4):
                    t_xe = cp([dx[3]], T.xe[:, 512 * c + 128 * k:512 * c + 128 * k + 128],
                              T.xr[:, 1536 + 128 * c:1536 + 128 * c + 128])
            for o in range(O):
                t_wq = quant([dw], T.wq, T.ws, 128 * o, 128, T.wr, 512 * o)
            for c in range(4):
                t_eq = quant([t_xe], T.eq, T.es, 128 * c, 128, T.xe, 512 * c)
        else:
            i = 4 * (b - 1)
            t_q = ts([t_m], T.mq4[:, i:i + 4], T.mx[:, i:i + 4], -0.25, None, OP.mult)
            if b < R - 1:
                t_st = tt([t_q, t_st], T.st[:, 4 * b:4 * b + 4], T.mq4[:, i:i + 4], T.st[:, i:i + 4], OP.add)
            else:
                t_st = tt([t_q, t_st, t_sf], T.sf[:, 0:4], T.mq4[:, i:i + 4], T.st[:, i:i + 4], OP.add)
                t_sft = turn([t_st], T.sft[:], T.sf[:])
                for a in range(4):
                    outs.append(dma("Y", T.se[0:1, 128 * a:128 * a + 128], T.sft[32 * a:32 * a + 4, :], "dout", [t_sft]))

        arrived = [("arr%d" % b, (N - 1) * 2 * engs), t_pk, t_psc]
        if b < R - 1:
            t_mm = [mm(arrived + [free_c[c]], T.psc[:, 512 * c:512 * c + 128], 128 * c, T.pq, T.ps, 128 * b, T.mq, T.ms, 128)
                    for c in range(4)]
            t_red = [None] * 4
            nb = B + 128
            t_b4 = [None] * 4
            for c in range(4):
                i = 4 * b + c
                m1, s1, out = T.mx[:, i:i + 1], T.srp[:, i:i + 1], T.bc[:, nb + 32 * c:nb + 32 * c + 32]
                t_red[c] = rmax([t_mm[c]], m1, T.psc[:, 512 * c:512 * c + 128])
                if c < 3:
                    t_b4[c] = act([t_red[c], t_srp, t_quart], out, T.quart[:], AF.Identity, bias=s1, scale=m1)
                else:
                    t_b4[c] = ts([t_red[c]], out, T.quart[:], m1, s1, OP.mult, OP.add)
            turn([t_b4[2]], T.srt[:, nb:nb + 96], T.bc[:, nb:nb + 96])
            t_srt = turn([t_b4[3]], T.srt[:, nb + 96:nb + 128], T.bc[:, nb + 96:nb + 128])
            t_m = t_red[3]
            t_ext = [mm([t_red[c], t_eq], T.psc[:, 512 * c:512 * c + 128], 128 * c, T.eq, T.es, 128 * b, T.mq, T.ms, 128)
                     for c in range(4)]
        for o in range(O):
            t_y[o] = mm(arrived + [t_wq] + ([free_y[o]] if free_y[o] else []), T.psy[:, 512 * o:512 * o + 128],
                        128 * o, T.wq, T.ws, 128 * b, T.mq, T.ms, 128)
        if b == R - 1:
            store(b, 0, "V")
            store(b, 1, "S")

    need("Y", [outs[-1]])
    need("G", [("loc", 2 * R * engs)])
    for s in ("sv", "ss", "sp", "sg"):
        need("Y", [(s, count[s])])
